import numpy as np
import ml_dtypes


def mxq(x, axis, fmt="e4m3"):
    dtype, down = {"e4m3": (ml_dtypes.float8_e4m3fn, 7), "e5m2": (ml_dtypes.float8_e5m2, 14)}[fmt]
    v = np.moveaxis(np.asarray(x, np.float32).astype(ml_dtypes.bfloat16).astype(np.float64), axis, -1)
    blocks = v.reshape(v.shape[:-1] + (-1, 32))
    amax = np.abs(blocks).max(-1, keepdims=True)
    byte = np.maximum(np.where(amax > 0, np.frexp(amax)[1] - 1 + 127, 0) - down, 1)
    scale = np.exp2(byte - 127.0)
    codes = (blocks / scale).astype(np.float32).astype(dtype).astype(np.float64)
    return np.moveaxis((codes * scale).reshape(v.shape), -1, axis)


WIDE = False


def mx_kscale(k):
    if not WIDE:
        return np.ones(k)
    levels = np.array([10, -10, 5, -5, 0])
    if k % 512:
        return np.exp2(np.random.permutation(np.resize(levels, k // 32))).repeat(32)
    a = np.empty((k // 512, 16))
    for p in range(k // 512):
        a[p, :8] = np.random.permutation(np.resize(levels, 8))
        for g in range(8):
            far = levels[np.abs(levels - a[p, g]) >= 10]
            a[p, g + 8] = far[np.random.randint(len(far))]
    return np.exp2(a.ravel()).repeat(32)


def f64(x):
    return np.asarray(x).astype(np.float64)


def striped(idx):
    return np.tile(np.asarray(idx).reshape(-1, 16).T, (8, 1)).astype(np.uint16)


def unstriped(offs):
    return offs[:16].T.reshape(-1).astype(np.int64)


E2M1 = np.array([0.0, 0.5, 1.0, 1.5, 2.0, 3.0, 4.0, 6.0, -0.0, -0.5, -1.0, -1.5, -2.0, -3.0, -4.0, -6.0])


def pack_weight(w, fmt):
    k, n = w.shape
    w = f64(np.asarray(w, np.float32).astype(ml_dtypes.bfloat16)).reshape(k // 32, 32, n)
    amax = np.abs(w).max(1)
    if fmt == "e4m3":
        byte = np.frexp(amax)[1] - 1 + 127 - 7
    else:
        mant, ex = np.frexp(amax / 6.0)
        byte = np.where(mant > 0.5, ex, ex - 1) + 127
    byte = np.clip(np.where(amax > 0, byte, 1), 1, 254)
    scaled = (w * np.exp2(127.0 - byte)[:, None, :]).reshape(k, n).astype(np.float32)
    by_word = np.ascontiguousarray(scaled.reshape(k // 512, 128, 4, n).transpose(0, 1, 3, 2))
    if fmt == "e4m3":
        words = by_word.astype(ml_dtypes.float8_e4m3fn).view(np.uint8)
    else:
        c = by_word.astype(ml_dtypes.float4_e2m1fn).view(np.uint8) & 0xF
        words = (c[..., 0::2] | (c[..., 1::2] << 4)).reshape(k // 512, 128, 2 * n)
    return np.ascontiguousarray(words), np.ascontiguousarray(byte.astype(np.uint8).reshape(k // 512, 16, n))


def unpack_weight(words, scales, fmt):
    g, _, n = scales.shape
    words = np.ascontiguousarray(words).reshape(g, 128, n, -1)
    if fmt == "e4m3":
        vals = words.view(ml_dtypes.float8_e4m3fn).astype(np.float64)
    else:
        nib = np.empty((g, 128, n, 4), np.uint8)
        nib[..., 0::2] = words & 0xF
        nib[..., 1::2] = words >> 4
        vals = E2M1[nib]
    vals = vals * np.repeat(np.exp2(scales.astype(np.float64) - 127.0), 8, axis=1)[..., None]
    return vals.transpose(0, 1, 3, 2).reshape(g * 512, n)


def bf(x):
    return np.asarray(x, np.float32).astype(ml_dtypes.bfloat16)


def planes(Y):
    r, m = Y.shape
    b = f64(bf(Y)).reshape(r // 32, 32, m)
    amax = np.abs(b).max(1)
    byte = np.clip(np.where(amax > 0, np.frexp(amax)[1] - 1 + 127 - 7, 1), 1, 254)
    codes = (b * np.exp2(127.0 - byte)[:, None, :]).reshape(r, m).astype(np.float32).astype(ml_dtypes.float8_e4m3fn).view(np.uint8)
    words = codes.reshape(r // 512, 128, 4, m).transpose(0, 1, 3, 2)
    return np.ascontiguousarray(words), np.ascontiguousarray(byte.astype(np.uint8).reshape(r // 512, 16, m))


D, T, I, Q, E, M, C = 512, 2048, 512, 256, 512, 1024, 512


def setup_inputs():
    n = np.random.standard_normal
    idx = np.random.permutation(T)[:I]
    idx2 = np.random.permutation(T)[:I]
    idx3 = np.random.permutation(M)[:Q]
    fd = mx_kscale(D)
    fi = mx_kscale(I)
    fc = mx_kscale(C)
    ti = np.ones(T)
    ti[idx] = fi
    keysp = pack_weight(n((D, T)) / fd[:, None], "e2m1")
    return {
        "query": (n((D, Q)) * 1.0 / np.sqrt(D) * fd[:, None]).astype(np.float32),
        "keys_words": keysp[0],
        "keys_scales": keysp[1],
        "os": (np.random.uniform(0.02, 0.08, (1, I)) * fi).astype(np.float32),
        "vals": (n((E, T)) / ti).astype(np.float32),
        "wm": (n((C, E)) * 1.0 / np.sqrt(C) * fc[:, None]).astype(np.float32),
        "mstore": (n((C, M)) / fc[:, None]).astype(np.float32),
        "offs": striped(idx),
        "offs2": striped(idx2),
        "offs3": striped(idx3),
    }


def reference(query, keys_words, keys_scales, os, vals, wm, mstore, offs, offs2, offs3):
    idx = unstriped(offs)
    idx2 = unstriped(offs2)
    idx3 = unstriped(offs3)
    keysu = unpack_weight(keys_words, keys_scales, "e2m1")
    queryq = mxq(f64(query), 0, "e4m3")
    a = queryq.T @ keysu
    s = a[:, idx] - a[:, idx2]
    w = np.maximum(s, 0.0)
    wo1 = w * f64(os)
    wt1 = wo1.T
    vt1 = f64(vals)[:, idx].T
    vt1q = mxq(vt1, 0, "e4m3")
    wt1q = mxq(wt1, 0, "e4m3")
    o = vt1q.T @ wt1q
    wmq = mxq(f64(wm), 0, "e4m3")
    mstoreq = mxq(f64(mstore), 0, "e4m3")
    me = wmq.T @ mstoreq
    y = np.maximum(o, me[:, idx3])
    words, scales = planes(y)
    return y, words, scales

@@ -1,0 +1,340 @@
+from contextlib import ExitStack
+
+import concourse.mybir as mybir
+from concourse.masks import make_identity
+
+D, T, I, Q, E, M, C = 512, 2048, 512, 256, 512, 1024, 512
+FLOPS = 2 * (Q * D * T + E * I * Q + E * C * M)
+
+F32 = mybir.dt.float32
+BF16 = mybir.dt.bfloat16
+I32 = mybir.dt.int32
+U32 = mybir.dt.uint32
+U16 = mybir.dt.uint16
+U8 = mybir.dt.uint8
+FP8X4 = mybir.dt.float8_e4m3fn_x4
+FP4X4 = mybir.dt.float4_e2m1fn_x4
+ALU = mybir.AluOpType
+COPY = mybir.ActivationFunctionType.Copy
+
+P = 128
+PACK = 4
+BANK = 512
+TAGS = {"plus0":"ms_bf1","diff0":"ms_raw2","diff1":"ms_bf2"}
+OFFS = {"v_raw1":0,"v_raw2":8192,"v_raw3":16384,"w_bf":0,"mem":8192,"v_bf0":12288,"v_bf1":13312,"v_bf2":16384,"v_bf3":17408,"v_codes0":18432,"v_codes1":18944}
+
+
+def tile_attend_difference_memorylarger_lean_pl_kernel(
+    tc, query, keys_words, keys_scales, slot_factor, vals, wm, mstore, offs, offs2, offs3, out_0, out_1, out_2
+):
+    nc = tc.nc
+    S, V, G = "scalar", "vector", "gpsimd"
+    with ExitStack() as ctx:
+        sb = ctx.enter_context(tc.tile_pool(name="sb", bufs=1))
+        ps = ctx.enter_context(tc.psum_pool(name="ps", bufs=1))
+
+        shared = ctx.enter_context(tc.tile_pool(name="shared", bufs=1))
+
+        def new(name, shape, dtype):
+            if name in OFFS:
+                return shared.tile(shape, dtype, name=name, align_bytes=64, offset=OFFS[name])
+            return sb.tile(shape, dtype, name=name, tag=TAGS.get(name, name), align_bytes=64)
+
+        def bank(number, shape):
+            return ps.tile(shape, F32, name="bank%d" % number)
+
+        def quantize(codes, scales, grouped):
+            nc.vector.quantize_mx(out=codes.bitcast(FP8X4), scales=scales, in_=grouped)
+
+        def cast(engine, out, in_):
+            if engine == V:
+                nc.vector.tensor_copy(out=out, in_=in_)
+            elif engine == S:
+                nc.scalar.copy(out=out, in_=in_)
+            else:
+                nc.gpsimd.tensor_scalar(out=out, in0=in_, scalar1=1.0, scalar2=0.0, op0=ALU.mult, op1=ALU.add)
+
+        def interleave(engine, grouped, raw):
+            cast(engine, grouped.rearrange("p (c i j) -> p c j i", i=4, j=PACK), raw.rearrange("p j (c i) -> p c j i", i=4))
+
+        def gather(engine, out, window):
+            if engine == S:
+                nc.scalar.activation(out, window, COPY)
+            else:
+                nc.vector.tensor_copy(out, window)
+
+        list1 = new("list1", [P, I // 16], U16)
+        list2 = new("list2", [P, I // 16], U16)
+        list3 = new("list3", [P, Q // 16], U16)
+        key_scales = new("key_scales", [P, T], U8)
+        nc.gpsimd.memset(key_scales[:].bitcast(I32), 0)
+        slot_f = new("slot_f", [P, PACK], F32)
+        nc.gpsimd.dma_start(out=slot_f[:], in_=slot_factor.rearrange("o (p j) -> p (o j)", j=PACK))
+        ident = new("ident", [P, P], F32)
+        make_identity(nc, ident[:])
+
+        def load(name, shape, source):
+            raw = new(name, shape, F32)
+            nc.sync.dma_start(out=raw[:], in_=source)
+            return raw
+
+        def load_keys(h):
+            words = new("key_words%d" % h, [P, T], U8)
+            nc.sync.dma_start(out=words[:].bitcast(I32), in_=keys_words[0, :, h * T : (h + 1) * T].bitcast(I32))
+            return words
+
+        wm_rows = wm.rearrange("(p j) e -> p j e", j=PACK)
+        ms_rows = mstore.rearrange("(p j) m -> p j m", j=PACK)
+        v_rows = vals.rearrange("(p j) t -> p j t", j=PACK)
+        q_raw = load("q_raw", [P, PACK, Q], query.rearrange("(p j) q -> p j q", j=PACK))
+        for quad in range(4):
+            nc.sync.dma_start(
+                out=key_scales[32 * quad : 32 * quad + 4, :].bitcast(I32),
+                in_=keys_scales[0, 4 * quad : 4 * quad + 4, :].bitcast(I32),
+            )
+        wm_raw = [load("wm_raw0", [P, PACK, 256], wm_rows[:, :, 0:256])]
+        key_words = [load_keys(0)]
+        wm_raw.append(load("wm_raw1", [P, PACK, 256], wm_rows[:, :, 256:512]))
+        key_words.append(load_keys(1))
+        nc.sync.dma_start(list1[:], offs)
+        nc.sync.dma_start(list2[:], offs2)
+        ms_raw = [
+            load("ms_raw0", [P, PACK, 256], ms_rows[:, :, 0:256]),
+            load("ms_raw1", [P, PACK, 256], ms_rows[:, :, 256:512]),
+            load("ms_raw2", [P, PACK, 512], ms_rows[:, :, 512:1024]),
+        ]
+        nc.sync.dma_start(list3[:], offs3)
+        v_raw = [load("v_raw%d" % j, [P, T], v_rows[:, j, :]) for j in range(PACK)]
+
+        q_codes, q_scales = new("q_codes", [P, Q], U32), new("q_scales", [P, Q], U8)
+        wm_codes, wm_scales = new("wm_codes", [P, E], U32), new("wm_scales", [P, E], U8)
+        ms_codes, ms_scales = new("ms_codes", [P, M], U32), new("ms_scales", [P, M], U8)
+        w_codes, w_scales = new("w_codes", [P, Q], U32), new("w_scales", [P, Q], U8)
+        wm_bf = new("wm_bf", [P, E * PACK], BF16)
+        w_bf = new("w_bf", [P, Q * PACK], BF16)
+        a_sb = [new("a%d" % b, [P, T], F32) for b in range(2)]
+        me_sb = [new("me%d" % j, [P, M], F32) for j in range(PACK)]
+        picked = [new("picked%d" % j, [P, I], BF16) for j in range(PACK)]
+        y = new("y", [P, PACK, Q], F32)
+        out_rows = out_0.rearrange("(p j) q -> p j q", j=PACK)
+        made = {}
+
+        def cq():
+            q_bf = new("q_bf", [P, Q * PACK], BF16)
+            interleave(V, q_bf[:], q_raw[:])
+            quantize(q_codes[:], q_scales[:], q_bf[:])
+
+        def a(b, n, engine, number):
+            rows = slice(b * P, (b + 1) * P)
+            cols = slice(n * BANK, (n + 1) * BANK)
+            acc = bank(number, [P, BANK])
+            nc.tensor.matmul_mx(
+                out=acc[:],
+                lhsT=q_codes[:, rows].bitcast(FP8X4),
+                lhsT_scale=q_scales[:, rows],
+                rhs=key_words[n // 2][:, (n % 2) * 1024 : (n % 2 + 1) * 1024].bitcast(FP4X4),
+                rhs_scale=key_scales[:, cols],
+                start=True,
+                stop=True,
+            )
+            cast(engine, a_sb[b][:, cols], acc[:])
+
+        def cwm(h, engine):
+            cast(
+                engine,
+                wm_bf[:].rearrange("p (t m j) -> p m j t", t=PACK, j=PACK)[:, 64 * h : 64 * (h + 1), :, :],
+                wm_raw[h][:].rearrange("p j (m t) -> p m j t", t=PACK),
+            )
+
+        def qwm():
+            quantize(wm_codes[:], wm_scales[:], wm_bf[:])
+
+        MS_COLS = [slice(0, 256), slice(256, 512), slice(512, 1024)]
+
+        def cm(h, engine):
+            width = MS_COLS[h].stop - MS_COLS[h].start
+            made["ms_bf", h] = new("ms_bf%d" % h, [P, width * PACK], BF16)
+            interleave(engine, made["ms_bf", h][:], ms_raw[h][:])
+
+        def qm(h):
+            quantize(ms_codes[:, MS_COLS[h]], ms_scales[:, MS_COLS[h]], made["ms_bf", h][:])
+
+        def emm(h, j, number):
+            rows = slice(j * P, (j + 1) * P)
+            cols = slice(h * BANK, (h + 1) * BANK)
+            acc = bank(number, [P, BANK])
+            nc.tensor.matmul_mx(
+                out=acc[:],
+                lhsT=wm_codes[:, rows].bitcast(FP8X4),
+                lhsT_scale=wm_scales[:, rows],
+                rhs=ms_codes[:, cols].bitcast(FP8X4),
+                rhs_scale=ms_scales[:, cols],
+                start=True,
+                stop=True,
+            )
+            made["e", h, j] = acc
+
+        def ce(h, j, engine):
+            cast(engine, me_sb[j][:, h * BANK : (h + 1) * BANK], made["e", h, j][:])
+
+        def pl(b, engine):
+            made["pl", b] = new("plus%d" % b, [P, I], F32)
+            gather(engine, made["pl", b][:], a_sb[b][:].indirect(list1[:]))
+
+        def mi(b, engine):
+            made["mi", b] = new("minus%d" % b, [P, I], F32)
+            gather(engine, made["mi", b][:], a_sb[b][:].indirect(list2[:]))
+
+        def sub(b):
+            made["s", b] = new("diff%d" % b, [P, PACK, P], F32)
+            nc.vector.tensor_tensor(
+                out=made["s", b][:].rearrange("p t s -> p s t"),
+                in0=made["pl", b][:].rearrange("p (s t) -> p s t", t=PACK),
+                in1=made["mi", b][:].rearrange("p (s t) -> p s t", t=PACK),
+                op=ALU.subtract,
+            )
+
+        def st(b, number):
+            made["st", b] = bank(number, [P, PACK, P])
+            for t in range(PACK):
+                nc.tensor.transpose(made["st", b][:, t, :], made["s", b][:, t, :], ident[:])
+
+        def w(b):
+            nc.vector.scalar_tensor_tensor(
+                out=w_bf[:, b * P * PACK : (b + 1) * P * PACK].rearrange("p (q t) -> p q t", t=PACK),
+                in0=made["st", b][:].rearrange("p t q -> p q t"),
+                scalar=0.0,
+                in1=slot_f[:].unsqueeze(1).to_broadcast([P, P, PACK]),
+                op0=ALU.max,
+                op1=ALU.mult,
+            )
+
+        def qw():
+            quantize(w_codes[:], w_scales[:], w_bf[:])
+
+        def g(j, engine, first, last):
+            gather(engine, picked[j][:, first:last], v_raw[j][:].indirect(list1[:, first // 16 : last // 16]))
+
+        def vt(j, number):
+            words = picked[j][:].bitcast(F32)
+            made["t", j] = bank(number, [P, 2, P])
+            for u in range(2):
+                nc.tensor.transpose(made["t", j][:, u, :], words[:, u::2], ident[:])
+
+        def ct(j, engine):
+            made["v_bf", j] = new("v_bf%d" % j, [P, P * PACK], BF16)
+            cast(engine, made["v_bf", j][:].bitcast(F32).rearrange("p (c u) -> p c u", u=2), made["t", j][:].rearrange("p u c -> p c u"))
+
+        def qv(j):
+            made["vq", j] = new("v_codes%d" % j, [P, P], U32), new("v_scales%d" % j, [P, P], U8)
+            quantize(made["vq", j][0][:], made["vq", j][1][:], made["v_bf", j][:])
+
+        def mg(j, engine):
+            if "mem" not in made:
+                made["mem"] = new("mem", [P, PACK, Q], F32)
+            gather(engine, made["mem"][:, j, :], me_sb[j][:].indirect(list3[:]))
+
+        def o(j, number):
+            made["o", j] = bank(number, [P, Q])
+            nc.tensor.matmul_mx(
+                out=made["o", j][:],
+                lhsT=made["vq", j][0][:].bitcast(FP8X4),
+                lhsT_scale=made["vq", j][1][:],
+                rhs=w_codes[:].bitcast(FP8X4),
+                rhs_scale=w_scales[:],
+                start=True,
+                stop=True,
+            )
+
+        def res(j):
+            nc.vector.tensor_tensor(out=y[:, j, :], in0=made["o", j][:], in1=made["mem"][:, j, :], op=ALU.max)
+            nc.sync.dma_start(out=out_rows[:, j, :], in_=y[:, j, :])
+
+        def fin():
+            y_bf = new("y_bf", [P, Q * PACK], BF16)
+            interleave(V, y_bf[:, 0 : 168 * PACK], y[:, :, 0:168])
+            interleave(S, y_bf[:, 168 * PACK :], y[:, :, 168:])
+            y_codes, y_scales = new("y_codes", [P, Q], U32), new("y_scales", [P, Q], U8)
+            quantize(y_codes[:], y_scales[:], y_bf[:])
+            nc.sync.dma_start(out=out_1[0].rearrange("p c r -> p (c r)").bitcast(I32), in_=y_codes[:].bitcast(I32))
+            for quad in range(4):
+                queue = nc.scalar if quad % 2 == 0 else nc.sync
+                queue.dma_start(
+                    out=out_2[0, 4 * quad : 4 * quad + 4, :].bitcast(I32),
+                    in_=y_scales[32 * quad : 32 * quad + 4, :].bitcast(I32),
+                )
+
+        cq()
+        cwm(0, V)
+        a(0, 0, S, 0)
+        a(0, 1, S, 1)
+        a(1, 0, S, 2)
+        a(1, 1, S, 3)
+        cwm(1, V)
+        qwm()
+        a(0, 2, S, 4)
+        a(0, 3, S, 5)
+        a(1, 2, S, 6)
+        a(1, 3, S, 7)
+        cm(0, V)
+        qm(0)
+        cm(1, V)
+        qm(1)
+        emm(0, 0, 0)
+        emm(0, 1, 1)
+        emm(0, 2, 2)
+        emm(0, 3, 3)
+        pl(0, V)
+        mi(0, S)
+        cm(2, V)
+        qm(2)
+        emm(1, 0, 4)
+        emm(1, 1, 5)
+        emm(1, 2, 6)
+        emm(1, 3, 7)
+        pl(1, S)
+        mi(1, S)
+        sub(0)
+        ce(0, 0, S)
+        st(0, 0)
+        sub(1)
+        ce(0, 1, S)
+        st(1, 1)
+        ce(0, 2, S)
+        ce(0, 3, S)
+        g(1, V, 0, 512)
+        g(0, S, 0, 512)
+        vt(0, 2)
+        vt(1, 3)
+        ce(1, 0, V)
+        w(0)
+        w(1)
+        ce(1, 1, V)
+        ce(1, 2, S)
+        ce(1, 3, S)
+        qw()
+        g(2, S, 0, 512)
+        vt(2, 4)
+        g(3, V, 0, 512)
+        vt(3, 5)
+        ct(0, S)
+        ct(1, S)
+        qv(0)
+        o(0, 6)
+        qv(1)
+        o(1, 7)
+        ct(2, V)
+        mg(0, S)
+        ct(3, V)
+        qv(2)
+        o(2, 0)
+        mg(1, S)
+        qv(3)
+        o(3, 1)
+        mg(2, S)
+        res(0)
+        mg(3, S)
+        res(1)
+        res(2)
+        res(3)
+        fin()

@@ -20,8 +20,8 @@ COPY = mybir.ActivationFunctionType.Copy
 P = 128
 PACK = 4
 BANK = 512
-TAGS = {"plus0":"ms_bf1","diff0":"ms_raw2","diff1":"ms_bf2"}
-OFFS = {"v_raw1":0,"v_raw2":8192,"v_raw3":16384,"w_bf":0,"mem":8192,"v_bf0":12288,"v_bf1":13312,"v_bf2":16384,"v_bf3":17408,"v_codes0":18432,"v_codes1":18944}
+TAGS = {"plus0":"wm_bf","diff0":"ms_raw1","diff1":"ms_bf1"}
+OFFS = {"v_raw1":0,"v_raw2":8192,"v_raw3":16384,"w_bf":0,"v_bf0":2048,"v_bf1":3072,"mem0":8192,"y":16384,"mem1":20480,"mem2":21504,"mem3":22528,"v_codes2":23552}
 
 
 def tile_attend_difference_memorylarger_lean_pl_kernel(
@@ -69,7 +69,6 @@ def tile_attend_difference_memorylarger_lean_pl_kernel(
         key_scales = new("key_scales", [P, T], U8)
         nc.gpsimd.memset(key_scales[:].bitcast(I32), 0)
         slot_f = new("slot_f", [P, PACK], F32)
-        nc.gpsimd.dma_start(out=slot_f[:], in_=slot_factor.rearrange("o (p j) -> p (o j)", j=PACK))
         ident = new("ident", [P, P], F32)
         make_identity(nc, ident[:])
 
@@ -77,11 +76,6 @@ def tile_attend_difference_memorylarger_lean_pl_kernel(
             raw = new(name, shape, F32)
             nc.sync.dma_start(out=raw[:], in_=source)
             return raw
-
-        def load_keys(h):
-            words = new("key_words%d" % h, [P, T], U8)
-            nc.sync.dma_start(out=words[:].bitcast(I32), in_=keys_words[0, :, h * T : (h + 1) * T].bitcast(I32))
-            return words
 
         wm_rows = wm.rearrange("(p j) e -> p j e", j=PACK)
         ms_rows = mstore.rearrange("(p j) m -> p j m", j=PACK)
@@ -92,19 +86,16 @@ def tile_attend_difference_memorylarger_lean_pl_kernel(
                 out=key_scales[32 * quad : 32 * quad + 4, :].bitcast(I32),
                 in_=keys_scales[0, 4 * quad : 4 * quad + 4, :].bitcast(I32),
             )
-        wm_raw = [load("wm_raw0", [P, PACK, 256], wm_rows[:, :, 0:256])]
-        key_words = [load_keys(0)]
-        wm_raw.append(load("wm_raw1", [P, PACK, 256], wm_rows[:, :, 256:512]))
-        key_words.append(load_keys(1))
+        key_words = new("key_words", [P, 2 * T], U8)
+        nc.sync.dma_start(out=key_words[:].bitcast(I32), in_=keys_words[0].bitcast(I32))
+        wm_raw = load("wm_raw", [P, PACK, E], wm_rows)
         nc.sync.dma_start(list1[:], offs)
         nc.sync.dma_start(list2[:], offs2)
-        ms_raw = [
-            load("ms_raw0", [P, PACK, 256], ms_rows[:, :, 0:256]),
-            load("ms_raw1", [P, PACK, 256], ms_rows[:, :, 256:512]),
-            load("ms_raw2", [P, PACK, 512], ms_rows[:, :, 512:1024]),
-        ]
+        ms_raw = [load("ms_raw%d" % h, [P, PACK, BANK], ms_rows[:, :, h * BANK : (h + 1) * BANK]) for h in range(2)]
+        v_raw = [load("v_raw0", [P, T], v_rows[:, 0, :])]
         nc.sync.dma_start(list3[:], offs3)
-        v_raw = [load("v_raw%d" % j, [P, T], v_rows[:, j, :]) for j in range(PACK)]
+        nc.sync.dma_start(out=slot_f[:], in_=slot_factor.rearrange("o (p j) -> p (o j)", j=PACK))
+        v_raw.extend(load("v_raw%d" % j, [P, T], v_rows[:, j, :]) for j in range(1, PACK))
 
         q_codes, q_scales = new("q_codes", [P, Q], U32), new("q_scales", [P, Q], U8)
         wm_codes, wm_scales = new("wm_codes", [P, E], U32), new("wm_scales", [P, E], U8)
@@ -132,7 +123,7 @@ def tile_attend_difference_memorylarger_lean_pl_kernel(
                 out=acc[:],
                 lhsT=q_codes[:, rows].bitcast(FP8X4),
                 lhsT_scale=q_scales[:, rows],
-                rhs=key_words[n // 2][:, (n % 2) * 1024 : (n % 2 + 1) * 1024].bitcast(FP4X4),
+                rhs=key_words[:, 2 * n * BANK : 2 * (n + 1) * BANK].bitcast(FP4X4),
                 rhs_scale=key_scales[:, cols],
                 start=True,
                 stop=True,
@@ -142,14 +133,14 @@ def tile_attend_difference_memorylarger_lean_pl_kernel(
         def cwm(h, engine):
             cast(
                 engine,
-                wm_bf[:].rearrange("p (t m j) -> p m j t", t=PACK, j=PACK)[:, 64 * h : 64 * (h + 1), :, :],
-                wm_raw[h][:].rearrange("p j (m t) -> p m j t", t=PACK),
+                wm_bf[:].rearrange("p (t m j) -> p m j t", t=PACK, j=PACK),
+                wm_raw[:].rearrange("p j (m t) -> p m j t", t=PACK),
             )
 
         def qwm():
             quantize(wm_codes[:], wm_scales[:], wm_bf[:])
 
-        MS_COLS = [slice(0, 256), slice(256, 512), slice(512, 1024)]
+        MS_COLS = [slice(0, 512), slice(512, 1024)]
 
         def cm(h, engine):
             width = MS_COLS[h].stop - MS_COLS[h].start
@@ -230,14 +221,15 @@ def tile_attend_difference_memorylarger_lean_pl_kernel(
             quantize(made["vq", j][0][:], made["vq", j][1][:], made["v_bf", j][:])
 
         def mg(j, engine):
-            if "mem" not in made:
-                made["mem"] = new("mem", [P, PACK, Q], F32)
-            gather(engine, made["mem"][:, j, :], me_sb[j][:].indirect(list3[:]))
+            made["mem", j] = new("mem%d" % j, [P, Q], F32)
+            gather(engine, made["mem", j][:], me_sb[j][:].indirect(list3[:]))
 
         def o(j, number):
-            made["o", j] = bank(number, [P, Q])
+            if j == 0:
+                made["o01"] = bank(number, [P, 2, Q])
+            made["o", j] = made["o01"][:, j, :] if j < 2 else bank(number, [P, Q])[:]
             nc.tensor.matmul_mx(
-                out=made["o", j][:],
+                out=made["o", j],
                 lhsT=made["vq", j][0][:].bitcast(FP8X4),
                 lhsT_scale=made["vq", j][1][:],
                 rhs=w_codes[:].bitcast(FP8X4),
@@ -247,7 +239,7 @@ def tile_attend_difference_memorylarger_lean_pl_kernel(
             )
 
         def res(j):
-            nc.vector.tensor_tensor(out=y[:, j, :], in0=made["o", j][:], in1=made["mem"][:, j, :], op=ALU.max)
+            nc.vector.tensor_tensor(out=y[:, j, :], in0=made["o", j], in1=made["mem", j][:], op=ALU.max)
             nc.sync.dma_start(out=out_rows[:, j, :], in_=y[:, j, :])
 
         def fin():
@@ -265,29 +257,26 @@ def tile_attend_difference_memorylarger_lean_pl_kernel(
                 )
 
         cq()
-        cwm(0, V)
         a(0, 0, S, 0)
-        a(0, 1, S, 1)
-        a(1, 0, S, 2)
-        a(1, 1, S, 3)
-        cwm(1, V)
+        a(0, 1, V, 1)
+        a(0, 2, S, 2)
+        a(0, 3, S, 3)
+        cwm(0, V)
         qwm()
-        a(0, 2, S, 4)
-        a(0, 3, S, 5)
+        a(1, 0, S, 4)
+        a(1, 1, S, 5)
         a(1, 2, S, 6)
         a(1, 3, S, 7)
+        pl(0, V)
+        mi(0, S)
         cm(0, V)
         qm(0)
-        cm(1, V)
-        qm(1)
         emm(0, 0, 0)
         emm(0, 1, 1)
         emm(0, 2, 2)
         emm(0, 3, 3)
-        pl(0, V)
-        mi(0, S)
-        cm(2, V)
-        qm(2)
+        cm(1, V)
+        qm(1)
         emm(1, 0, 4)
         emm(1, 1, 5)
         emm(1, 2, 6)
@@ -302,39 +291,40 @@ def tile_attend_difference_memorylarger_lean_pl_kernel(
         st(1, 1)
         ce(0, 2, S)
         ce(0, 3, S)
-        g(1, V, 0, 512)
+        ce(1, 0, V)
+        ce(1, 1, V)
         g(0, S, 0, 512)
+        g(1, V, 0, 512)
         vt(0, 2)
         vt(1, 3)
-        ce(1, 0, V)
         w(0)
         w(1)
-        ce(1, 1, V)
         ce(1, 2, S)
         ce(1, 3, S)
         qw()
+        ct(0, V)
+        ct(1, V)
         g(2, S, 0, 512)
         vt(2, 4)
-        g(3, V, 0, 512)
-        vt(3, 5)
-        ct(0, S)
-        ct(1, S)
         qv(0)
-        o(0, 6)
         qv(1)
-        o(1, 7)
-        ct(2, V)
         mg(0, S)
-        ct(3, V)
+        ct(2, S)
+        o(0, 4)
+        o(1, 7)
+        g(3, S, 0, 256)
+        g(3, V, 256, 512)
+        vt(3, 5)
         qv(2)
         o(2, 0)
         mg(1, S)
+        res(0)
+        ct(3, V)
+        mg(2, S)
         qv(3)
         o(3, 1)
-        mg(2, S)
-        res(0)
-        mg(3, S)
         res(1)
+        mg(3, S)
         res(2)
         res(3)
         fin()

@@ -20,311 +20,293 @@ COPY = mybir.ActivationFunctionType.Copy
 P = 128
 PACK = 4
 BANK = 512
-TAGS = {"plus0":"wm_bf","diff0":"ms_raw1","diff1":"ms_bf1"}
-OFFS = {"v_raw1":0,"v_raw2":8192,"v_raw3":16384,"w_bf":0,"v_bf0":2048,"v_bf1":3072,"mem0":8192,"y":16384,"mem1":20480,"mem2":21504,"mem3":22528,"v_codes2":23552}
+LINE = 4
+PER_COLUMN = 16
+VECTOR_COLUMNS = 136
+
+KIB = 1024
+PLACES = {
+    "wm_bf": 0,
+    "plus0": 0,
+    "ms_raw1": 4 * KIB,
+    "diff0": 4 * KIB,
+    "diff1": 6 * KIB,
+    "v_raw1": 12 * KIB,
+    "w_bf": 12 * KIB,
+    "v_bf01": 14 * KIB,
+    "v_raw2": 20 * KIB,
+    "mem0": 20 * KIB,
+    "v_raw3": 28 * KIB,
+    "y": 28 * KIB,
+    "mem1": 32 * KIB,
+    "mem2": 33 * KIB,
+    "v_bf2": 34 * KIB,
+    "picked3": 36 * KIB,
+    "mem3": 36 * KIB,
+}
 
 
 def tile_attend_difference_memorylarger_lean_pl_kernel(
     tc, query, keys_words, keys_scales, slot_factor, vals, wm, mstore, offs, offs2, offs3, out_0, out_1, out_2
 ):
     nc = tc.nc
-    S, V, G = "scalar", "vector", "gpsimd"
+    on_vector, on_scalar = nc.vector.tensor_copy, nc.scalar.copy
     with ExitStack() as ctx:
-        sb = ctx.enter_context(tc.tile_pool(name="sb", bufs=1))
-        ps = ctx.enter_context(tc.psum_pool(name="ps", bufs=1))
-
-        shared = ctx.enter_context(tc.tile_pool(name="shared", bufs=1))
+        held = ctx.enter_context(tc.tile_pool(name="held", bufs=1))
+        reused = ctx.enter_context(tc.tile_pool(name="reused", bufs=1))
+        psum = ctx.enter_context(tc.psum_pool(name="psum", bufs=1))
 
         def new(name, shape, dtype):
-            if name in OFFS:
-                return shared.tile(shape, dtype, name=name, align_bytes=64, offset=OFFS[name])
-            return sb.tile(shape, dtype, name=name, tag=TAGS.get(name, name), align_bytes=64)
+            if name in PLACES:
+                return reused.tile(shape, dtype, name=name, align_bytes=64, offset=PLACES[name])
+            return held.tile(shape, dtype, name=name, align_bytes=64)
 
         def bank(number, shape):
-            return ps.tile(shape, F32, name="bank%d" % number)
+            return psum.tile(shape, F32, name="bank%d" % number)
 
-        def quantize(codes, scales, grouped):
-            nc.vector.quantize_mx(out=codes.bitcast(FP8X4), scales=scales, in_=grouped)
+        def operand(name, width):
+            return new(name + "_codes", [P, width], U32), new(name + "_scales", [P, width], U8)
 
-        def cast(engine, out, in_):
-            if engine == V:
-                nc.vector.tensor_copy(out=out, in_=in_)
-            elif engine == S:
-                nc.scalar.copy(out=out, in_=in_)
-            else:
-                nc.gpsimd.tensor_scalar(out=out, in0=in_, scalar1=1.0, scalar2=0.0, op0=ALU.mult, op1=ALU.add)
+        def quantize(target, cols, grouped):
+            codes, scales = target
+            nc.vector.quantize_mx(out=codes[:, cols].bitcast(FP8X4), scales=scales[:, cols], in_=grouped)
 
-        def interleave(engine, grouped, raw):
-            cast(engine, grouped.rearrange("p (c i j) -> p c j i", i=4, j=PACK), raw.rearrange("p j (c i) -> p c j i", i=4))
+        def interleave(copy, grouped, rows):
+            copy(
+                out=grouped.rearrange("p (c i r) -> p c r i", i=LINE, r=PACK),
+                in_=rows.rearrange("p r (c i) -> p c r i", i=LINE),
+            )
 
-        def gather(engine, out, window):
-            if engine == S:
+        def round_and_quantize(name, raw, target, first):
+            half = raw.shape[2] // 2
+            grouped = new(name + "_bf", [P, 2, half * PACK], BF16)
+            for h in range(2):
+                interleave(on_vector, grouped[:, h, :], raw[:, :, h * half : (h + 1) * half])
+            for h in range(2):
+                quantize(target, slice(first + h * half, first + (h + 1) * half), grouped[:, h, :])
+
+        def product(out, stationary, rows, moving_codes, moving_scales):
+            codes, scales = stationary
+            nc.tensor.matmul_mx(
+                out=out,
+                lhsT=codes[:, rows].bitcast(FP8X4),
+                lhsT_scale=scales[:, rows],
+                rhs=moving_codes,
+                rhs_scale=moving_scales,
+                start=True,
+                stop=True,
+            )
+
+        def look_up(copy, out, window):
+            if copy is on_scalar:
                 nc.scalar.activation(out, window, COPY)
             else:
                 nc.vector.tensor_copy(out, window)
 
-        list1 = new("list1", [P, I // 16], U16)
-        list2 = new("list2", [P, I // 16], U16)
-        list3 = new("list3", [P, Q // 16], U16)
+        list1 = new("list1", [P, I // PER_COLUMN], U16)
+        list2 = new("list2", [P, I // PER_COLUMN], U16)
+        list3 = new("list3", [P, Q // PER_COLUMN], U16)
         key_scales = new("key_scales", [P, T], U8)
         nc.gpsimd.memset(key_scales[:].bitcast(I32), 0)
-        slot_f = new("slot_f", [P, PACK], F32)
-        ident = new("ident", [P, P], F32)
-        make_identity(nc, ident[:])
+        identity = new("identity", [P, P], F32)
+        make_identity(nc, identity[:])
 
         def load(name, shape, source):
             raw = new(name, shape, F32)
             nc.sync.dma_start(out=raw[:], in_=source)
             return raw
 
-        wm_rows = wm.rearrange("(p j) e -> p j e", j=PACK)
-        ms_rows = mstore.rearrange("(p j) m -> p j m", j=PACK)
-        v_rows = vals.rearrange("(p j) t -> p j t", j=PACK)
-        q_raw = load("q_raw", [P, PACK, Q], query.rearrange("(p j) q -> p j q", j=PACK))
-        for quad in range(4):
+        q_raw = load("q_raw", [P, PACK, Q], query.rearrange("(p r) q -> p r q", r=PACK))
+        for quadrant in range(4):
             nc.sync.dma_start(
-                out=key_scales[32 * quad : 32 * quad + 4, :].bitcast(I32),
-                in_=keys_scales[0, 4 * quad : 4 * quad + 4, :].bitcast(I32),
+                out=key_scales[32 * quadrant : 32 * quadrant + 4, :].bitcast(I32),
+                in_=keys_scales[0, 4 * quadrant : 4 * quadrant + 4, :].bitcast(I32),
             )
         key_words = new("key_words", [P, 2 * T], U8)
         nc.sync.dma_start(out=key_words[:].bitcast(I32), in_=keys_words[0].bitcast(I32))
-        wm_raw = load("wm_raw", [P, PACK, E], wm_rows)
+        wm_raw = load("wm_raw", [P, PACK, E], wm.rearrange("(p r) e -> p r e", r=PACK))
         nc.sync.dma_start(list1[:], offs)
         nc.sync.dma_start(list2[:], offs2)
+        ms_rows = mstore.rearrange("(p r) m -> p r m", r=PACK)
         ms_raw = [load("ms_raw%d" % h, [P, PACK, BANK], ms_rows[:, :, h * BANK : (h + 1) * BANK]) for h in range(2)]
-        v_raw = [load("v_raw0", [P, T], v_rows[:, 0, :])]
+        v_planes = vals.rearrange("(p j) t -> p j t", j=PACK)
+        v_raw = [load("v_raw0", [P, T], v_planes[:, 0, :])]
         nc.sync.dma_start(list3[:], offs3)
-        nc.sync.dma_start(out=slot_f[:], in_=slot_factor.rearrange("o (p j) -> p (o j)", j=PACK))
-        v_raw.extend(load("v_raw%d" % j, [P, T], v_rows[:, j, :]) for j in range(1, PACK))
+        slot_f = load("slot_f", [P, PACK], slot_factor.rearrange("o (p r) -> p (o r)", r=PACK))
+        v_raw.extend(load("v_raw%d" % j, [P, T], v_planes[:, j, :]) for j in range(1, PACK))
 
-        q_codes, q_scales = new("q_codes", [P, Q], U32), new("q_scales", [P, Q], U8)
-        wm_codes, wm_scales = new("wm_codes", [P, E], U32), new("wm_scales", [P, E], U8)
-        ms_codes, ms_scales = new("ms_codes", [P, M], U32), new("ms_scales", [P, M], U8)
-        w_codes, w_scales = new("w_codes", [P, Q], U32), new("w_scales", [P, Q], U8)
-        wm_bf = new("wm_bf", [P, E * PACK], BF16)
-        w_bf = new("w_bf", [P, Q * PACK], BF16)
-        a_sb = [new("a%d" % b, [P, T], F32) for b in range(2)]
+        q_op, wm_op, ms_op, w_op = operand("q", Q), operand("wm", E), operand("ms", M), operand("w", Q)
+        a_sb = [new("a%d" % b, [P, T], F32) for b in range(Q // P)]
         me_sb = [new("me%d" % j, [P, M], F32) for j in range(PACK)]
-        picked = [new("picked%d" % j, [P, I], BF16) for j in range(PACK)]
-        y = new("y", [P, PACK, Q], F32)
-        out_rows = out_0.rearrange("(p j) q -> p j q", j=PACK)
-        made = {}
+        out_planes = out_0.rearrange("(p j) q -> p j q", j=PACK)
 
-        def cq():
-            q_bf = new("q_bf", [P, Q * PACK], BF16)
-            interleave(V, q_bf[:], q_raw[:])
-            quantize(q_codes[:], q_scales[:], q_bf[:])
-
-        def a(b, n, engine, number):
-            rows = slice(b * P, (b + 1) * P)
+        def scores(b, n, number, copy):
             cols = slice(n * BANK, (n + 1) * BANK)
             acc = bank(number, [P, BANK])
-            nc.tensor.matmul_mx(
-                out=acc[:],
-                lhsT=q_codes[:, rows].bitcast(FP8X4),
-                lhsT_scale=q_scales[:, rows],
-                rhs=key_words[:, 2 * n * BANK : 2 * (n + 1) * BANK].bitcast(FP4X4),
-                rhs_scale=key_scales[:, cols],
-                start=True,
-                stop=True,
-            )
-            cast(engine, a_sb[b][:, cols], acc[:])
+            words = key_words[:, 2 * n * BANK : 2 * (n + 1) * BANK].bitcast(FP4X4)
+            product(acc[:], q_op, slice(b * P, (b + 1) * P), words, key_scales[:, cols])
+            copy(out=a_sb[b][:, cols], in_=acc[:])
 
-        def cwm(h, engine):
-            cast(
-                engine,
-                wm_bf[:].rearrange("p (t m j) -> p m j t", t=PACK, j=PACK),
-                wm_raw[:].rearrange("p j (m t) -> p m j t", t=PACK),
-            )
-
-        def qwm():
-            quantize(wm_codes[:], wm_scales[:], wm_bf[:])
-
-        MS_COLS = [slice(0, 512), slice(512, 1024)]
-
-        def cm(h, engine):
-            width = MS_COLS[h].stop - MS_COLS[h].start
-            made["ms_bf", h] = new("ms_bf%d" % h, [P, width * PACK], BF16)
-            interleave(engine, made["ms_bf", h][:], ms_raw[h][:])
-
-        def qm(h):
-            quantize(ms_codes[:, MS_COLS[h]], ms_scales[:, MS_COLS[h]], made["ms_bf", h][:])
-
-        def emm(h, j, number):
-            rows = slice(j * P, (j + 1) * P)
+        def memories(h, first_bank):
+            round_and_quantize("ms%d" % h, ms_raw[h], ms_op, h * BANK)
             cols = slice(h * BANK, (h + 1) * BANK)
-            acc = bank(number, [P, BANK])
-            nc.tensor.matmul_mx(
-                out=acc[:],
-                lhsT=wm_codes[:, rows].bitcast(FP8X4),
-                lhsT_scale=wm_scales[:, rows],
-                rhs=ms_codes[:, cols].bitcast(FP8X4),
-                rhs_scale=ms_scales[:, cols],
-                start=True,
-                stop=True,
-            )
-            made["e", h, j] = acc
+            banks = [bank(first_bank + j, [P, BANK]) for j in range(PACK)]
+            for j in range(PACK):
+                product(banks[j][:], wm_op, slice(j * P, (j + 1) * P), ms_op[0][:, cols].bitcast(FP8X4), ms_op[1][:, cols])
+            return banks
 
-        def ce(h, j, engine):
-            cast(engine, me_sb[j][:, h * BANK : (h + 1) * BANK], made["e", h, j][:])
+        def keep_memories(h, j, banks, copy):
+            copy(out=me_sb[j][:, h * BANK : (h + 1) * BANK], in_=banks[j][:])
 
-        def pl(b, engine):
-            made["pl", b] = new("plus%d" % b, [P, I], F32)
-            gather(engine, made["pl", b][:], a_sb[b][:].indirect(list1[:]))
+        def score_look_up(name, b, offsets, copy):
+            picked_scores = new("%s%d" % (name, b), [P, I], F32)
+            look_up(copy, picked_scores[:], a_sb[b][:].indirect(offsets[:]))
+            return picked_scores
 
-        def mi(b, engine):
-            made["mi", b] = new("minus%d" % b, [P, I], F32)
-            gather(engine, made["mi", b][:], a_sb[b][:].indirect(list2[:]))
-
-        def sub(b):
-            made["s", b] = new("diff%d" % b, [P, PACK, P], F32)
+        def difference(b, plus, minus):
+            diff = new("diff%d" % b, [P, PACK, P], F32)
             nc.vector.tensor_tensor(
-                out=made["s", b][:].rearrange("p t s -> p s t"),
-                in0=made["pl", b][:].rearrange("p (s t) -> p s t", t=PACK),
-                in1=made["mi", b][:].rearrange("p (s t) -> p s t", t=PACK),
+                out=diff[:].rearrange("p r n -> p n r"),
+                in0=plus[:].rearrange("p (n r) -> p n r", r=PACK),
+                in1=minus[:].rearrange("p (n r) -> p n r", r=PACK),
                 op=ALU.subtract,
             )
+            return diff
 
-        def st(b, number):
-            made["st", b] = bank(number, [P, PACK, P])
-            for t in range(PACK):
-                nc.tensor.transpose(made["st", b][:, t, :], made["s", b][:, t, :], ident[:])
+        def turn_scores(diff, number):
+            turned = bank(number, [P, PACK, P])
+            for r in range(PACK):
+                nc.tensor.transpose(turned[:, r, :], diff[:, r, :], identity[:])
+            return turned
 
-        def w(b):
+        def weigh(b, turned):
             nc.vector.scalar_tensor_tensor(
-                out=w_bf[:, b * P * PACK : (b + 1) * P * PACK].rearrange("p (q t) -> p q t", t=PACK),
-                in0=made["st", b][:].rearrange("p t q -> p q t"),
+                out=w_bf[:, b * P * PACK : (b + 1) * P * PACK].rearrange("p (q r) -> p q r", r=PACK),
+                in0=turned[:].rearrange("p r q -> p q r"),
                 scalar=0.0,
                 in1=slot_f[:].unsqueeze(1).to_broadcast([P, P, PACK]),
                 op0=ALU.max,
                 op1=ALU.mult,
             )
 
-        def qw():
-            quantize(w_codes[:], w_scales[:], w_bf[:])
+        def value_look_up(j, copy, first, last):
+            window = v_raw[j][:].indirect(list1[:, first // PER_COLUMN : last // PER_COLUMN])
+            look_up(copy, picked[j][:, first:last], window)
 
-        def g(j, engine, first, last):
-            gather(engine, picked[j][:, first:last], v_raw[j][:].indirect(list1[:, first // 16 : last // 16]))
-
-        def vt(j, number):
+        def turn_values(j, turned):
             words = picked[j][:].bitcast(F32)
-            made["t", j] = bank(number, [P, 2, P])
             for u in range(2):
-                nc.tensor.transpose(made["t", j][:, u, :], words[:, u::2], ident[:])
+                nc.tensor.transpose(turned[:, u, :], words[:, u::2], identity[:])
 
-        def ct(j, engine):
-            made["v_bf", j] = new("v_bf%d" % j, [P, P * PACK], BF16)
-            cast(engine, made["v_bf", j][:].bitcast(F32).rearrange("p (c u) -> p c u", u=2), made["t", j][:].rearrange("p u c -> p c u"))
-
-        def qv(j):
-            made["vq", j] = new("v_codes%d" % j, [P, P], U32), new("v_scales%d" % j, [P, P], U8)
-            quantize(made["vq", j][0][:], made["vq", j][1][:], made["v_bf", j][:])
-
-        def mg(j, engine):
-            made["mem", j] = new("mem%d" % j, [P, Q], F32)
-            gather(engine, made["mem", j][:], me_sb[j][:].indirect(list3[:]))
-
-        def o(j, number):
-            if j == 0:
-                made["o01"] = bank(number, [P, 2, Q])
-            made["o", j] = made["o01"][:, j, :] if j < 2 else bank(number, [P, Q])[:]
-            nc.tensor.matmul_mx(
-                out=made["o", j],
-                lhsT=made["vq", j][0][:].bitcast(FP8X4),
-                lhsT_scale=made["vq", j][1][:],
-                rhs=w_codes[:].bitcast(FP8X4),
-                rhs_scale=w_scales[:],
-                start=True,
-                stop=True,
+        def keep_values(name, turned, copy):
+            planes = turned.shape[1]
+            grouped = new("v_bf" + name, [P, planes * P * PACK], BF16)
+            copy(
+                out=grouped[:].bitcast(F32).rearrange("p (n c u) -> p n c u", n=planes, u=2),
+                in_=turned[:].rearrange("p n u c -> p n c u"),
             )
+            return grouped
 
-        def res(j):
-            nc.vector.tensor_tensor(out=y[:, j, :], in0=made["o", j], in1=made["mem", j][:], op=ALU.max)
-            nc.sync.dma_start(out=out_rows[:, j, :], in_=y[:, j, :])
+        def value_operand(name, grouped):
+            width = grouped.shape[1] // PACK
+            target = operand("v" + name, width)
+            quantize(target, slice(0, width), grouped[:])
+            return target
 
-        def fin():
-            y_bf = new("y_bf", [P, Q * PACK], BF16)
-            interleave(V, y_bf[:, 0 : 168 * PACK], y[:, :, 0:168])
-            interleave(S, y_bf[:, 168 * PACK :], y[:, :, 168:])
-            y_codes, y_scales = new("y_codes", [P, Q], U32), new("y_scales", [P, Q], U8)
-            quantize(y_codes[:], y_scales[:], y_bf[:])
-            nc.sync.dma_start(out=out_1[0].rearrange("p c r -> p (c r)").bitcast(I32), in_=y_codes[:].bitcast(I32))
-            for quad in range(4):
-                queue = nc.scalar if quad % 2 == 0 else nc.sync
-                queue.dma_start(
-                    out=out_2[0, 4 * quad : 4 * quad + 4, :].bitcast(I32),
-                    in_=y_scales[32 * quad : 32 * quad + 4, :].bitcast(I32),
-                )
+        def weighted_values(target, number):
+            planes = target[0].shape[1] // P
+            acc = bank(number, [P, planes, Q])
+            for n in range(planes):
+                product(acc[:, n, :], target, slice(n * P, (n + 1) * P), w_op[0][:].bitcast(FP8X4), w_op[1][:])
+            return acc
 
-        cq()
-        a(0, 0, S, 0)
-        a(0, 1, V, 1)
-        a(0, 2, S, 2)
-        a(0, 3, S, 3)
-        cwm(0, V)
-        qwm()
-        a(1, 0, S, 4)
-        a(1, 1, S, 5)
-        a(1, 2, S, 6)
-        a(1, 3, S, 7)
-        pl(0, V)
-        mi(0, S)
-        cm(0, V)
-        qm(0)
-        emm(0, 0, 0)
-        emm(0, 1, 1)
-        emm(0, 2, 2)
-        emm(0, 3, 3)
-        cm(1, V)
-        qm(1)
-        emm(1, 0, 4)
-        emm(1, 1, 5)
-        emm(1, 2, 6)
-        emm(1, 3, 7)
-        pl(1, S)
-        mi(1, S)
-        sub(0)
-        ce(0, 0, S)
-        st(0, 0)
-        sub(1)
-        ce(0, 1, S)
-        st(1, 1)
-        ce(0, 2, S)
-        ce(0, 3, S)
-        ce(1, 0, V)
-        ce(1, 1, V)
-        g(0, S, 0, 512)
-        g(1, V, 0, 512)
-        vt(0, 2)
-        vt(1, 3)
-        w(0)
-        w(1)
-        ce(1, 2, S)
-        ce(1, 3, S)
-        qw()
-        ct(0, V)
-        ct(1, V)
-        g(2, S, 0, 512)
-        vt(2, 4)
-        qv(0)
-        qv(1)
-        mg(0, S)
-        ct(2, S)
-        o(0, 4)
-        o(1, 7)
-        g(3, S, 0, 256)
-        g(3, V, 256, 512)
-        vt(3, 5)
-        qv(2)
-        o(2, 0)
-        mg(1, S)
-        res(0)
-        ct(3, V)
-        mg(2, S)
-        qv(3)
-        o(3, 1)
-        res(1)
-        mg(3, S)
-        res(2)
-        res(3)
-        fin()
+        def memory_look_up(j, copy):
+            mem = new("mem%d" % j, [P, Q], F32)
+            look_up(copy, mem[:], me_sb[j][:].indirect(list3[:]))
+            return mem
+
+        def result(j, o_plane, mem):
+            nc.vector.tensor_tensor(out=y[:, j, :], in0=o_plane, in1=mem[:], op=ALU.max)
+            nc.sync.dma_start(out=out_planes[:, j, :], in_=y[:, j, :])
+
+        round_and_quantize("q", q_raw, q_op, 0)
+        for n in range(T // BANK):
+            scores(0, n, n, on_vector if n == 1 else on_scalar)
+
+        wm_bf = new("wm_bf", [P, E * PACK], BF16)
+        nc.vector.tensor_copy(
+            out=wm_bf[:].rearrange("p (j m r) -> p m r j", j=PACK, r=PACK),
+            in_=wm_raw[:].rearrange("p r (m j) -> p m r j", j=PACK),
+        )
+        quantize(wm_op, slice(0, E), wm_bf[:])
+        for n in range(T // BANK):
+            scores(1, n, PACK + n, on_scalar)
+
+        plus0 = score_look_up("plus", 0, list1, on_vector)
+        minus0 = score_look_up("minus", 0, list2, on_scalar)
+        me_low = memories(0, 0)
+        me_high = memories(1, PACK)
+        plus1 = score_look_up("plus", 1, list1, on_scalar)
+        minus1 = score_look_up("minus", 1, list2, on_scalar)
+
+        diff0 = difference(0, plus0, minus0)
+        keep_memories(0, 0, me_low, on_scalar)
+        s_turned0 = turn_scores(diff0, 0)
+        diff1 = difference(1, plus1, minus1)
+        keep_memories(0, 1, me_low, on_scalar)
+        s_turned1 = turn_scores(diff1, 1)
+        keep_memories(0, 2, me_low, on_scalar)
+        keep_memories(0, 3, me_low, on_scalar)
+        keep_memories(1, 0, me_high, on_vector)
+        keep_memories(1, 1, me_high, on_vector)
+
+        picked = [new("picked%d" % j, [P, I], BF16) for j in range(PACK)]
+        value_look_up(0, on_scalar, 0, I)
+        value_look_up(1, on_vector, 0, I)
+        v_turned01 = bank(2, [P, 2, 2, P])
+        turn_values(0, v_turned01[:, 0, :, :])
+        turn_values(1, v_turned01[:, 1, :, :])
+        w_bf = new("w_bf", [P, Q * PACK], BF16)
+        weigh(0, s_turned0)
+        weigh(1, s_turned1)
+        keep_memories(1, 2, me_high, on_scalar)
+        keep_memories(1, 3, me_high, on_scalar)
+        v_bf01 = keep_values("01", v_turned01, on_vector)
+        quantize(w_op, slice(0, Q), w_bf[:])
+
+        value_look_up(2, on_scalar, 0, I)
+        v_turned2 = bank(4, [P, 1, 2, P])
+        turn_values(2, v_turned2[:, 0, :, :])
+        v_op01 = value_operand("01", v_bf01)
+        mem0 = memory_look_up(0, on_scalar)
+        value_look_up(3, on_scalar, 0, I // 2)
+        value_look_up(3, on_vector, I // 2, I)
+        v_turned3 = bank(5, [P, 1, 2, P])
+        turn_values(3, v_turned3[:, 0, :, :])
+
+        y = new("y", [P, PACK, Q], F32)
+        v_bf2 = keep_values("2", v_turned2, on_vector)
+        o01 = weighted_values(v_op01, 4)
+        mem2 = memory_look_up(2, on_scalar)
+        v_bf3 = keep_values("3", v_turned3, on_scalar)
+        o2 = weighted_values(value_operand("2", v_bf2), 0)
+        mem1 = memory_look_up(1, on_vector)
+        o3 = weighted_values(value_operand("3", v_bf3), 1)
+        result(0, o01[:, 0, :], mem0)
+        mem3 = memory_look_up(3, on_scalar)
+        result(1, o01[:, 1, :], mem1)
+        result(2, o2[:, 0, :], mem2)
+        result(3, o3[:, 0, :], mem3)
+
+        y_bf = new("y_bf", [P, Q * PACK], BF16)
+        interleave(on_vector, y_bf[:, : VECTOR_COLUMNS * PACK], y[:, :, :VECTOR_COLUMNS])
+        interleave(on_scalar, y_bf[:, VECTOR_COLUMNS * PACK :], y[:, :, VECTOR_COLUMNS:])
+        y_codes, y_scales = operand("y", Q)
+        quantize((y_codes, y_scales), slice(0, Q), y_bf[:])
+        nc.sync.dma_start(out=out_1[0].rearrange("p c r -> p (c r)").bitcast(I32), in_=y_codes[:].bitcast(I32))
+        for quadrant in range(4):
+            queue = nc.scalar if quadrant % 2 == 0 else nc.sync
+            queue.dma_start(
+                out=out_2[0, 4 * quadrant : 4 * quadrant + 4, :].bitcast(I32),
+                in_=y_scales[32 * quadrant : 32 * quadrant + 4, :].bitcast(I32),
+            )

from contextlib import ExitStack

import concourse.mybir as mybir
from concourse.masks import make_identity

D, T, I, Q, E, M, C = 512, 2048, 512, 256, 512, 1024, 512
FLOPS = 2 * (Q * D * T + E * I * Q + E * C * M)

F32 = mybir.dt.float32
BF16 = mybir.dt.bfloat16
I32 = mybir.dt.int32
U32 = mybir.dt.uint32
U16 = mybir.dt.uint16
U8 = mybir.dt.uint8
FP8X4 = mybir.dt.float8_e4m3fn_x4
FP4X4 = mybir.dt.float4_e2m1fn_x4
ALU = mybir.AluOpType
COPY = mybir.ActivationFunctionType.Copy

P = 128
PACK = 4
BANK = 512
LINE = 4
PER_COLUMN = 16
VECTOR_COLUMNS = 136

KIB = 1024
PLACES = {
    "wm_bf": 0,
    "plus0": 0,
    "ms_raw1": 4 * KIB,
    "diff0": 4 * KIB,
    "diff1": 6 * KIB,
    "v_raw1": 12 * KIB,
    "w_bf": 12 * KIB,
    "v_bf01": 14 * KIB,
    "v_raw2": 20 * KIB,
    "mem0": 20 * KIB,
    "v_raw3": 28 * KIB,
    "y": 28 * KIB,
    "mem1": 32 * KIB,
    "mem2": 33 * KIB,
    "v_bf2": 34 * KIB,
    "picked3": 36 * KIB,
    "mem3": 36 * KIB,
}


def tile_attend_difference_memorylarger_lean_pl_kernel(
    tc, query, keys_words, keys_scales, slot_factor, vals, wm, mstore, offs, offs2, offs3, out_0, out_1, out_2
):
    nc = tc.nc
    on_vector, on_scalar = nc.vector.tensor_copy, nc.scalar.copy
    with ExitStack() as ctx:
        held = ctx.enter_context(tc.tile_pool(name="held", bufs=1))
        reused = ctx.enter_context(tc.tile_pool(name="reused", bufs=1))
        psum = ctx.enter_context(tc.psum_pool(name="psum", bufs=1))

        def new(name, shape, dtype):
            if name in PLACES:
                return reused.tile(shape, dtype, name=name, align_bytes=64, offset=PLACES[name])
            return held.tile(shape, dtype, name=name, align_bytes=64)

        def bank(number, shape):
            return psum.tile(shape, F32, name="bank%d" % number)

        def operand(name, width):
            return new(name + "_codes", [P, width], U32), new(name + "_scales", [P, width], U8)

        def quantize(target, cols, grouped):
            codes, scales = target
            nc.vector.quantize_mx(out=codes[:, cols].bitcast(FP8X4), scales=scales[:, cols], in_=grouped)

        def interleave(copy, grouped, rows):
            copy(
                out=grouped.rearrange("p (c i r) -> p c r i", i=LINE, r=PACK),
                in_=rows.rearrange("p r (c i) -> p c r i", i=LINE),
            )

        def round_and_quantize(name, raw, target, first):
            half = raw.shape[2] // 2
            grouped = new(name + "_bf", [P, 2, half * PACK], BF16)
            for h in range(2):
                interleave(on_vector, grouped[:, h, :], raw[:, :, h * half : (h + 1) * half])
            for h in range(2):
                quantize(target, slice(first + h * half, first + (h + 1) * half), grouped[:, h, :])

        def product(out, stationary, rows, moving_codes, moving_scales):
            codes, scales = stationary
            nc.tensor.matmul_mx(
                out=out,
                lhsT=codes[:, rows].bitcast(FP8X4),
                lhsT_scale=scales[:, rows],
                rhs=moving_codes,
                rhs_scale=moving_scales,
                start=True,
                stop=True,
            )

        def look_up(copy, out, window):
            if copy is on_scalar:
                nc.scalar.activation(out, window, COPY)
            else:
                nc.vector.tensor_copy(out, window)

        list1 = new("list1", [P, I // PER_COLUMN], U16)
        list2 = new("list2", [P, I // PER_COLUMN], U16)
        list3 = new("list3", [P, Q // PER_COLUMN], U16)
        key_scales = new("key_scales", [P, T], U8)
        nc.gpsimd.memset(key_scales[:].bitcast(I32), 0)
        identity = new("identity", [P, P], F32)
        make_identity(nc, identity[:])

        def load(name, shape, source):
            raw = new(name, shape, F32)
            nc.sync.dma_start(out=raw[:], in_=source)
            return raw

        q_raw = load("q_raw", [P, PACK, Q], query.rearrange("(p r) q -> p r q", r=PACK))
        for quadrant in range(4):
            nc.sync.dma_start(
                out=key_scales[32 * quadrant : 32 * quadrant + 4, :].bitcast(I32),
                in_=keys_scales[0, 4 * quadrant : 4 * quadrant + 4, :].bitcast(I32),
            )
        key_words = new("key_words", [P, 2 * T], U8)
        nc.sync.dma_start(out=key_words[:].bitcast(I32), in_=keys_words[0].bitcast(I32))
        wm_raw = load("wm_raw", [P, PACK, E], wm.rearrange("(p r) e -> p r e", r=PACK))
        nc.sync.dma_start(list1[:], offs)
        nc.sync.dma_start(list2[:], offs2)
        ms_rows = mstore.rearrange("(p r) m -> p r m", r=PACK)
        ms_raw = [load("ms_raw%d" % h, [P, PACK, BANK], ms_rows[:, :, h * BANK : (h + 1) * BANK]) for h in range(2)]
        v_planes = vals.rearrange("(p j) t -> p j t", j=PACK)
        v_raw = [load("v_raw0", [P, T], v_planes[:, 0, :])]
        nc.sync.dma_start(list3[:], offs3)
        slot_f = load("slot_f", [P, PACK], slot_factor.rearrange("o (p r) -> p (o r)", r=PACK))
        v_raw.extend(load("v_raw%d" % j, [P, T], v_planes[:, j, :]) for j in range(1, PACK))

        q_op, wm_op, ms_op, w_op = operand("q", Q), operand("wm", E), operand("ms", M), operand("w", Q)
        a_sb = [new("a%d" % b, [P, T], F32) for b in range(Q // P)]
        me_sb = [new("me%d" % j, [P, M], F32) for j in range(PACK)]
        out_planes = out_0.rearrange("(p j) q -> p j q", j=PACK)

        def scores(b, n, number, copy):
            cols = slice(n * BANK, (n + 1) * BANK)
            acc = bank(number, [P, BANK])
            words = key_words[:, 2 * n * BANK : 2 * (n + 1) * BANK].bitcast(FP4X4)
            product(acc[:], q_op, slice(b * P, (b + 1) * P), words, key_scales[:, cols])
            copy(out=a_sb[b][:, cols], in_=acc[:])

        def memories(h, first_bank):
            round_and_quantize("ms%d" % h, ms_raw[h], ms_op, h * BANK)
            cols = slice(h * BANK, (h + 1) * BANK)
            banks = [bank(first_bank + j, [P, BANK]) for j in range(PACK)]
            for j in range(PACK):
                product(banks[j][:], wm_op, slice(j * P, (j + 1) * P), ms_op[0][:, cols].bitcast(FP8X4), ms_op[1][:, cols])
            return banks

        def keep_memories(h, j, banks, copy):
            copy(out=me_sb[j][:, h * BANK : (h + 1) * BANK], in_=banks[j][:])

        def score_look_up(name, b, offsets, copy):
            picked_scores = new("%s%d" % (name, b), [P, I], F32)
            look_up(copy, picked_scores[:], a_sb[b][:].indirect(offsets[:]))
            return picked_scores

        def difference(b, plus, minus):
            diff = new("diff%d" % b, [P, PACK, P], F32)
            nc.vector.tensor_tensor(
                out=diff[:].rearrange("p r n -> p n r"),
                in0=plus[:].rearrange("p (n r) -> p n r", r=PACK),
                in1=minus[:].rearrange("p (n r) -> p n r", r=PACK),
                op=ALU.subtract,
            )
            return diff

        def turn_scores(diff, number):
            turned = bank(number, [P, PACK, P])
            for r in range(PACK):
                nc.tensor.transpose(turned[:, r, :], diff[:, r, :], identity[:])
            return turned

        def weigh(b, turned):
            nc.vector.scalar_tensor_tensor(
                out=w_bf[:, b * P * PACK : (b + 1) * P * PACK].rearrange("p (q r) -> p q r", r=PACK),
                in0=turned[:].rearrange("p r q -> p q r"),
                scalar=0.0,
                in1=slot_f[:].unsqueeze(1).to_broadcast([P, P, PACK]),
                op0=ALU.max,
                op1=ALU.mult,
            )

        def value_look_up(j, copy, first, last):
            window = v_raw[j][:].indirect(list1[:, first // PER_COLUMN : last // PER_COLUMN])
            look_up(copy, picked[j][:, first:last], window)

        def turn_values(j, turned):
            words = picked[j][:].bitcast(F32)
            for u in range(2):
                nc.tensor.transpose(turned[:, u, :], words[:, u::2], identity[:])

        def keep_values(name, turned, copy):
            planes = turned.shape[1]
            grouped = new("v_bf" + name, [P, planes * P * PACK], BF16)
            copy(
                out=grouped[:].bitcast(F32).rearrange("p (n c u) -> p n c u", n=planes, u=2),
                in_=turned[:].rearrange("p n u c -> p n c u"),
            )
            return grouped

        def value_operand(name, grouped):
            width = grouped.shape[1] // PACK
            target = operand("v" + name, width)
            quantize(target, slice(0, width), grouped[:])
            return target

        def weighted_values(target, number):
            planes = target[0].shape[1] // P
            acc = bank(number, [P, planes, Q])
            for n in range(planes):
                product(acc[:, n, :], target, slice(n * P, (n + 1) * P), w_op[0][:].bitcast(FP8X4), w_op[1][:])
            return acc

        def memory_look_up(j, copy):
            mem = new("mem%d" % j, [P, Q], F32)
            look_up(copy, mem[:], me_sb[j][:].indirect(list3[:]))
            return mem

        def result(j, o_plane, mem):
            nc.vector.tensor_tensor(out=y[:, j, :], in0=o_plane, in1=mem[:], op=ALU.max)
            nc.sync.dma_start(out=out_planes[:, j, :], in_=y[:, j, :])

        round_and_quantize("q", q_raw, q_op, 0)
        for n in range(T // BANK):
            scores(0, n, n, on_vector if n == 1 else on_scalar)

        wm_bf = new("wm_bf", [P, E * PACK], BF16)
        nc.vector.tensor_copy(
            out=wm_bf[:].rearrange("p (j m r) -> p m r j", j=PACK, r=PACK),
            in_=wm_raw[:].rearrange("p r (m j) -> p m r j", j=PACK),
        )
        quantize(wm_op, slice(0, E), wm_bf[:])
        for n in range(T // BANK):
            scores(1, n, PACK + n, on_scalar)

        plus0 = score_look_up("plus", 0, list1, on_vector)
        minus0 = score_look_up("minus", 0, list2, on_scalar)
        me_low = memories(0, 0)
        me_high = memories(1, PACK)
        plus1 = score_look_up("plus", 1, list1, on_scalar)
        minus1 = score_look_up("minus", 1, list2, on_scalar)

        diff0 = difference(0, plus0, minus0)
        keep_memories(0, 0, me_low, on_scalar)
        s_turned0 = turn_scores(diff0, 0)
        diff1 = difference(1, plus1, minus1)
        keep_memories(0, 1, me_low, on_scalar)
        s_turned1 = turn_scores(diff1, 1)
        keep_memories(0, 2, me_low, on_scalar)
        keep_memories(0, 3, me_low, on_scalar)
        keep_memories(1, 0, me_high, on_vector)
        keep_memories(1, 1, me_high, on_vector)

        picked = [new("picked%d" % j, [P, I], BF16) for j in range(PACK)]
        value_look_up(0, on_scalar, 0, I)
        value_look_up(1, on_vector, 0, I)
        v_turned01 = bank(2, [P, 2, 2, P])
        turn_values(0, v_turned01[:, 0, :, :])
        turn_values(1, v_turned01[:, 1, :, :])
        w_bf = new("w_bf", [P, Q * PACK], BF16)
        weigh(0, s_turned0)
        weigh(1, s_turned1)
        keep_memories(1, 2, me_high, on_scalar)
        keep_memories(1, 3, me_high, on_scalar)
        v_bf01 = keep_values("01", v_turned01, on_vector)
        quantize(w_op, slice(0, Q), w_bf[:])

        value_look_up(2, on_scalar, 0, I)
        v_turned2 = bank(4, [P, 1, 2, P])
        turn_values(2, v_turned2[:, 0, :, :])
        v_op01 = value_operand("01", v_bf01)
        mem0 = memory_look_up(0, on_scalar)
        value_look_up(3, on_scalar, 0, I // 2)
        value_look_up(3, on_vector, I // 2, I)
        v_turned3 = bank(5, [P, 1, 2, P])
        turn_values(3, v_turned3[:, 0, :, :])

        y = new("y", [P, PACK, Q], F32)
        v_bf2 = keep_values("2", v_turned2, on_vector)
        o01 = weighted_values(v_op01, 4)
        mem2 = memory_look_up(2, on_scalar)
        v_bf3 = keep_values("3", v_turned3, on_scalar)
        o2 = weighted_values(value_operand("2", v_bf2), 0)
        mem1 = memory_look_up(1, on_vector)
        o3 = weighted_values(value_operand("3", v_bf3), 1)
        result(0, o01[:, 0, :], mem0)
        mem3 = memory_look_up(3, on_scalar)
        result(1, o01[:, 1, :], mem1)
        result(2, o2[:, 0, :], mem2)
        result(3, o3[:, 0, :], mem3)

        y_bf = new("y_bf", [P, Q * PACK], BF16)
        interleave(on_vector, y_bf[:, : VECTOR_COLUMNS * PACK], y[:, :, :VECTOR_COLUMNS])
        interleave(on_scalar, y_bf[:, VECTOR_COLUMNS * PACK :], y[:, :, VECTOR_COLUMNS:])
        y_codes, y_scales = operand("y", Q)
        quantize((y_codes, y_scales), slice(0, Q), y_bf[:])
        nc.sync.dma_start(out=out_1[0].rearrange("p c r -> p (c r)").bitcast(I32), in_=y_codes[:].bitcast(I32))
        for quadrant in range(4):
            queue = nc.scalar if quadrant % 2 == 0 else nc.sync
            queue.dma_start(
                out=out_2[0, 4 * quadrant : 4 * quadrant + 4, :].bitcast(I32),
                in_=y_scales[32 * quadrant : 32 * quadrant + 4, :].bitcast(I32),
            )
